import numpy as np
import ml_dtypes


def mxq(x, axis, fmt="e4m3"):
    dtype, down = {"e4m3": (ml_dtypes.float8_e4m3fn, 7), "e5m2": (ml_dtypes.float8_e5m2, 14)}[fmt]
    v = np.moveaxis(np.asarray(x, np.float32).astype(ml_dtypes.bfloat16).astype(np.float64), axis, -1)
    blocks = v.reshape(v.shape[:-1] + (-1, 32))
    amax = np.abs(blocks).max(-1, keepdims=True)
    byte = np.maximum(np.where(amax > 0, np.frexp(amax)[1] - 1 + 127, 0) - down, 1)
    scale = np.exp2(byte - 127.0)
    codes = (blocks / scale).astype(np.float32).astype(dtype).astype(np.float64)
    return np.moveaxis((codes * scale).reshape(v.shape), -1, axis)


WIDE = False


def mx_kscale(k):
    if not WIDE:
        return np.ones(k)
    levels = np.array([10, -10, 5, -5, 0])
    if k % 512:
        return np.exp2(np.random.permutation(np.resize(levels, k // 32))).repeat(32)
    a = np.empty((k // 512, 16))
    for p in range(k // 512):
        a[p, :8] = np.random.permutation(np.resize(levels, 8))
        for g in range(8):
            far = levels[np.abs(levels - a[p, g]) >= 10]
            a[p, g + 8] = far[np.random.randint(len(far))]
    return np.exp2(a.ravel()).repeat(32)


def f64(x):
    return np.asarray(x).astype(np.float64)


def striped(idx):
    return np.tile(np.asarray(idx).reshape(-1, 16).T, (8, 1)).astype(np.uint16)


def unstriped(offs):
    return offs[:16].T.reshape(-1).astype(np.int64)


B, N, T, D, DV, NQ = 1, 1024, 2048, 512, 128, 512


def setup_inputs():
    n = np.random.standard_normal
    idx = np.sort(np.random.permutation(T)[:B * N].reshape(B, N), axis=1).reshape(-1)
    s = mx_kscale(D)[:, None]
    u = np.ones(T)
    u[idx] = mx_kscale(B * N)
    r = np.random.uniform(0.5, 2.0, T)
    qidx = np.random.permutation(T)[:B * NQ]
    rk = np.random.uniform(0.5, 2.0, T)
    k = n((D, T)) / s / rk
    v = n((DV, T)) / (u * r)
    return {
        "xq": (n((D, T)) * s * (0.80 / np.sqrt(D))).astype(np.float32),
        "kT": k.astype(np.float32),
        "vT": v.astype(np.float32),
        "ks": np.tile(rk, (128, 1)).astype(np.float32),
        "vs": np.tile(u * r, (128, 1)).astype(np.float32),
        "offs": striped(idx),
        "qoffs": striped(qidx),
    }


def reference(xq, kT, vT, ks, vs, offs, qoffs):
    idx = unstriped(offs)
    k = f64(kT)
    v = f64(vT)
    pick = lambda x: x[:, idx].reshape(x.shape[0], B, N).transpose(1, 0, 2)
    q = f64(xq)[:, unstriped(qoffs)].reshape(D, B, NQ).transpose(1, 0, 2)
    score = mxq(q, 1, "e4m3").transpose(0, 2, 1) @ mxq(pick(k), 1, "e4m3")
    score = score * pick(f64(ks))[:, :1, :]
    m = score.max(-1, keepdims=True)
    p = np.exp(score - m)
    total = p.sum(-1, keepdims=True)
    w = p * pick(f64(vs))[:, :1, :]
    y = mxq(w, 2, "e4m3") @ mxq(pick(v).transpose(0, 2, 1), 1, "e4m3")
    y = y / total
    out = np.zeros((DV, T))
    out[:, unstriped(qoffs)] = y.transpose(2, 0, 1).reshape(-1, B * NQ)
    return out

@@ -1,0 +1,301 @@
+from contextlib import ExitStack
+
+import concourse.mybir as mybir
+from concourse.masks import make_identity
+
+P = 128
+D, T, N, NQ, DV = 512, 2048, 1024, 512, 128
+FLOPS = 2 * NQ * N * (D + DV)
+
+F32 = mybir.dt.float32
+BF16 = mybir.dt.bfloat16
+U32 = mybir.dt.uint32
+U16 = mybir.dt.uint16
+U8 = mybir.dt.uint8
+FP8X4 = mybir.dt.float8_e4m3fn_x4
+COPY = mybir.ActivationFunctionType.Copy
+EXP = mybir.ActivationFunctionType.Exp
+MULT = mybir.AluOpType.mult
+ADD = mybir.AluOpType.add
+MIN = mybir.AluOpType.min
+X = mybir.AxisListType.X
+
+
+def tile_attend_x_router_ks_kernel(tc, xq, kT, vT, ks, vs, offs, qoffs, out):
+    nc = tc.nc
+    with ExitStack() as ctx:
+        lists = ctx.enter_context(tc.tile_pool(name="lists", bufs=1))
+        keep = ctx.enter_context(tc.tile_pool(name="keep", bufs=1))
+        ring = ctx.enter_context(tc.tile_pool(name="ring", bufs=2))
+        banks = ctx.enter_context(tc.psum_pool(name="banks", bufs=1))
+
+        slots = lists.tile([P, N // 16], U16, name="slots")
+        nc.sync.dma_start(slots[:], offs)
+        qlist = lists.tile([P, NQ // 16], U16, name="qlist")
+        nc.sync.dma_start(qlist[:], qoffs)
+
+        ksw = keep.tile([P, T], F32, name="ksw")
+        vsw = keep.tile([P, T], F32, name="vsw")
+        warm = keep.tile([P, 1], F32, name="warm")
+        nc.vector.memset(warm[:], 0.0)
+        nc.vector.memset(ksw[:], 0.0)
+        nc.gpsimd.memset(vsw[:], 0.0)
+        nc.scalar.activation(warm[:], warm[:], EXP)
+
+        ident = keep.tile([P, P], F32, name="ident")
+        make_identity(nc, ident[:])
+        ident_bf16 = keep.tile([P, P], BF16, name="ident_bf16")
+        make_identity(nc, ident_bf16[:])
+
+        kview = kT.rearrange("(p t) w -> p t w", t=4)
+        qview = xq.rearrange("(p t) w -> p t w", t=4)
+        H = T // 2
+        raw = {}
+        for key, view, e in (("k0", kview, 0), ("k1", kview, 1), ("q0", qview, 0)):
+            r = keep.tile([P, 2, T], F32, name="raw_" + key)
+            for lo, hi in ((0, 512), (512, H), (H, T)) if key == "k0" else ((0, H), (H, T)):
+                nc.sync.dma_start(r[:, :, lo:hi], view[:, 2 * e : 2 * e + 2, lo:hi])
+                if key == "k0" and lo < H:
+                    scale_window, scale_input = (ksw, ks) if lo == 0 else (vsw, vs)
+                    nc.sync.dma_start(scale_window[0:1, :], scale_input[0:1, :])
+            raw[key] = r
+        qpl = {}
+        for t in (2, 3):
+            q_t = keep.tile([P, T], F32, name="qplane%d" % t)
+            nc.sync.dma_start(q_t[:], qview[:, t, :])
+            qpl[t] = q_t
+        vraw = keep.tile([P, T], F32, name="vraw")
+        nc.sync.dma_start(vraw[:], vT)
+
+        window = keep.tile([P, T], F32, name="window")
+        nc.gpsimd.memset(window[:], 0.0)
+
+        ksg = keep.tile([P, N], F32, name="ksg")
+        nc.vector.tensor_copy(ksg[:], ksw[:].indirect(slots[:]))
+        vsg = keep.tile([P, N], F32, name="vsg")
+        nc.vector.tensor_copy(vsg[:], vsw[:].indirect(slots[:]))
+        def to_column(name, gathered, factor):
+            col = keep.tile([P, 8], F32, name=name + "_col")
+            for g in range(2):
+                b = banks.tile([P, 4, P], F32, name="%s_b%d" % (name, g), tag="t", bufs=3)
+                for i in range(4):
+                    nc.tensor.transpose(b[:, i, :], gathered[:, (4 * g + i) * P : (4 * g + i + 1) * P], ident[:])
+                nc.vector.tensor_scalar(col[:, 4 * g : 4 * g + 4], b[:, :, 0], factor, None, MULT)
+            return col
+
+        def to_rows(name, col):
+            row = keep.tile([P, N], F32, name=name + "_row")
+            for g in range(2):
+                b = banks.tile([P, 4 * P], F32, name="%s_r%d" % (name, g), tag="t", bufs=3)
+                for i in range(4):
+                    c = 4 * g + i
+                    nc.tensor.transpose(b[:, i * P : (i + 1) * P], col[:, c : c + 1].to_broadcast([P, P]), ident[:])
+                nc.scalar.copy(row[:, g * 512 : (g + 1) * 512], b[:])
+            return row
+
+        nks_col = to_column("nks", ksg, -1.0)
+        vs_col = to_column("vs", vsg, 1.0)
+
+        kx = keep.tile([P, 4 * N], BF16, name="kx", align_bytes=64)
+        qx = keep.tile([P, 4 * NQ], BF16, name="qx", align_bytes=64)
+        pair = {}
+
+        def cast(key, lo, hi, engine):
+            dst = pair[key][:].rearrange("p (w e) -> p w e", e=2)[:, lo:hi, :]
+            src = raw[key][:, :, lo:hi].rearrange("p e w -> p w e")
+            if engine == "s":
+                nc.scalar.activation(dst, src, COPY)
+            else:
+                nc.vector.tensor_copy(dst, src)
+
+        def gather_pair(key, wide, e, offsets):
+            dst = wide[:].bitcast(U32).rearrange("p (n u) -> p n u", u=2)[:, :, e]
+            nc.vector.tensor_copy(dst, pair[key][:].bitcast(U32).indirect(offsets))
+
+        for key in ("k0", "k1", "q0"):
+            pair_tile = keep.tile([P, 2 * T], BF16, name="pair_" + key, align_bytes=64)
+            pair[key] = pair_tile
+        cast("k0", 0, 512, "s")
+        cast("k0", 512, H, "s")
+        cast("k0", H, T, "s")
+        gather_pair("k0", kx, 0, slots[:])
+        cast("k1", 0, H, "s")
+        cast("k1", H, H + H // 2, "s")
+        cast("k1", H + H // 2, T, "v")
+        gather_pair("k1", kx, 1, slots[:])
+        kc = keep.tile([P, N], U32, name="kc", align_bytes=64)
+        ksc = keep.tile([P, N], U8, name="ksc", align_bytes=64)
+        nc.vector.quantize_mx(out=kc[:].bitcast(FP8X4), scales=ksc[:], in_=kx[:])
+        cast("q0", 0, H, "s")
+        cast("q0", H, H + H // 2, "s")
+        cast("q0", H + H // 2, T, "v")
+        gather_pair("q0", qx, 0, qlist[:])
+        nks_row = to_rows("nks", nks_col)
+        vs_row = to_rows("vs", vs_col)
+        qc = keep.tile([P, NQ], U32, name="qc", align_bytes=64)
+        qsc = keep.tile([P, NQ], U8, name="qsc", align_bytes=64)
+
+        def gather_q(t, lo, hi):
+            dst = qx[:].rearrange("p (n f) -> p n f", f=4)[:, lo:hi, t]
+            nc.vector.tensor_copy(dst, qpl[t][:].indirect(qlist[:, lo // 16 : hi // 16]))
+
+        gather_q(2, 0, 512)
+        for h in range(2):
+            gather_q(3, h * 256, (h + 1) * 256)
+            nc.vector.quantize_mx(
+                out=qc[:, h * 256 : (h + 1) * 256].bitcast(FP8X4),
+                scales=qsc[:, h * 256 : (h + 1) * 256],
+                in_=qx[:, h * 1024 : (h + 1) * 1024],
+            )
+
+        nm = keep.tile([P, 4], F32, name="nm")
+        lparts = keep.tile([P, 4, 2], F32, name="lparts")
+        state = {}
+
+        def scores(j):
+            q_cols = slice(j * P, (j + 1) * P)
+            res = []
+            for g in range(2):
+                b = banks.tile([P, 512], F32, name="sc%d_%d" % (j, g), tag="s", bufs=4)
+                k_cols = slice(g * 512, (g + 1) * 512)
+                nc.tensor.matmul_mx(
+                    out=b[:],
+                    lhsT=qc[:, q_cols].bitcast(FP8X4),
+                    lhsT_scale=qsc[:, q_cols],
+                    rhs=kc[:, k_cols].bitcast(FP8X4),
+                    rhs_scale=ksc[:, k_cols],
+                    start=True,
+                    stop=True,
+                )
+                res.append(b)
+            state[j] = res
+
+        def scale_rows(j):
+            a = ring.tile([P, N], F32, name="a%d" % j, tag="a")
+            for g in range(2):
+                half = slice(g * 512, (g + 1) * 512)
+                nc.vector.tensor_tensor(a[:, half], state[j][g][:], nks_row[:, half], MULT)
+            nc.vector.tensor_reduce(nm[:, j : j + 1], a[:], X, MIN)
+            state[j] = [a[:, g * 512 : (g + 1) * 512] for g in range(2)]
+
+        def weights(j):
+            p = ring.tile([P, N], F32, name="p%d" % j, tag="p")
+            for g in range(2):
+                nc.scalar.activation(
+                    p[:, g * 512 : (g + 1) * 512],
+                    state[j][g],
+                    EXP,
+                    bias=nm[:, j : j + 1],
+                    scale=-1.0,
+                    accum_out=lparts[:, j, g : g + 1],
+                )
+            state[j] = p
+
+        def start_weights(j):
+            w = ring.tile([P, N], BF16, name="w%d" % j, tag="w")
+            wx = ring.tile([P, 2, 4 * P], BF16, name="wx%d" % j, tag="wx", align_bytes=64)
+            wc = ring.tile([P, 2 * P], U32, name="wc%d" % j, tag="wc", align_bytes=64)
+            wsc = ring.tile([P, 2 * P], U8, name="wsc%d" % j, tag="wsc", align_bytes=64)
+            state[j] = (state[j], w, wx, wc, wsc)
+
+        def scale_weights(j, g, engine):
+            p, w, wx, wc, wsc = state[j]
+            half = slice(g * 512, (g + 1) * 512)
+            engine.tensor_tensor(w[:, half], p[:, half], vs_row[:, half], MULT)
+
+        def turn_weights(j, g, copy):
+            p, w, wx, wc, wsc = state[j]
+            words = w[:, g * 512 : (g + 1) * 512].bitcast(F32)
+            b = banks.tile([P, 2, P], F32, name="pt%d_%d" % (j, g), tag="t", bufs=3)
+            for u in range(2):
+                nc.tensor.transpose(b[:, u, :], words[:, u::2], ident[:])
+            copy(wx[:, g, :].bitcast(F32).rearrange("p (q u) -> p q u", u=2), b[:].rearrange("p u q -> p q u"))
+
+        def quantise_weights(j, g):
+            p, w, wx, wc, wsc = state[j]
+            cols = slice(g * P, (g + 1) * P)
+            nc.vector.quantize_mx(out=wc[:, cols].bitcast(FP8X4), scales=wsc[:, cols], in_=wx[:, g, :])
+
+        ybank = banks.tile([P, NQ], F32, name="ybank", tag="y", bufs=1)
+
+        def values(j):
+            p, w, wx, wc, wsc = state[j]
+            for g in range(2):
+                cols = slice(g * P, (g + 1) * P)
+                nc.tensor.matmul_mx(
+                    out=ybank[:, j * P : (j + 1) * P],
+                    lhsT=vc[:, cols].bitcast(FP8X4),
+                    lhsT_scale=vsc[:, cols],
+                    rhs=wc[:, cols].bitcast(FP8X4),
+                    rhs_scale=wsc[:, cols],
+                    start=(g == 0),
+                    stop=(g == 1),
+                )
+
+        y_sb = keep.tile([P, NQ], F32, name="y_sb")
+        rl_sb = keep.tile([P, NQ], F32, name="rl_sb")
+        rl = keep.tile([P, 4], F32, name="rl")
+        lsum = keep.tile([P, 4], F32, name="lsum")
+
+        def scatter(h):
+            js = slice(2 * h, 2 * h + 2)
+            nc.gpsimd.tensor_tensor(lsum[:, js], lparts[:, js, 0], lparts[:, js, 1], ADD)
+            nc.vector.reciprocal(rl[:, js], lsum[:, js])
+            b = banks.tile([P, 256], F32, name="rlb%d" % h, tag="t", bufs=3)
+            for i in range(2):
+                c = 2 * h + i
+                nc.tensor.transpose(b[:, i * P : (i + 1) * P], rl[:, c : c + 1].to_broadcast([P, P]), ident[:])
+            cols = slice(h * 256, (h + 1) * 256)
+            nc.scalar.copy(rl_sb[:, cols], b[:])
+            nc.scalar.copy(y_sb[:, cols], ybank[:, cols])
+            nc.vector.tensor_tensor(
+                window[:].indirect(qlist[:, h * 16 : (h + 1) * 16]), y_sb[:, cols], rl_sb[:, cols], MULT
+            )
+
+        for j in range(4):
+            scores(j)
+
+        vb = keep.tile([P, T], BF16, name="vb")
+        for i in range(4):
+            nc.scalar.activation(vb[:, i * 512 : (i + 1) * 512], vraw[:, i * 512 : (i + 1) * 512], COPY)
+        vg = keep.tile([P, N, 2], BF16, name="vg")
+        for g in range(2):
+            nc.scalar.activation(
+                vg[:, g * 512 : (g + 1) * 512, 0], vb[:].indirect(slots[:, g * 32 : (g + 1) * 32]), COPY
+            )
+        vx = keep.tile([P, 2, DV, 4], BF16, name="vx", align_bytes=64)
+        for g in range(2):
+            b = banks.tile([P, 4, DV], BF16, name="vt%d" % g, tag="t", bufs=3)
+            for t in range(4):
+                nc.tensor.transpose(b[:, t, :], vg[:, g * 512 + t : (g + 1) * 512 : 4, 0], ident_bf16[:])
+            nc.scalar.copy(vx[:, g, :, :], b[:].rearrange("p t e -> p e t"))
+        vc = keep.tile([P, 2 * DV], U32, name="vc", align_bytes=64)
+        vsc = keep.tile([P, 2 * DV], U8, name="vsc", align_bytes=64)
+
+        def finish(j, engine):
+            start_weights(j)
+            for g in range(2):
+                scale_weights(j, g, engine)
+                turn_weights(j, g, nc.scalar.copy)
+                quantise_weights(j, g)
+            if j == 0:
+                nc.vector.quantize_mx(
+                    out=vc[:].bitcast(FP8X4), scales=vsc[:], in_=vx[:].rearrange("p g e t -> p (g e t)")
+                )
+            values(j)
+
+        scale_rows(0)
+        weights(0)
+        scale_rows(1)
+        weights(1)
+        finish(0, nc.gpsimd)
+        scale_rows(2)
+        weights(2)
+        finish(1, nc.gpsimd)
+        scale_rows(3)
+        weights(3)
+        scatter(0)
+        finish(2, nc.gpsimd)
+        finish(3, nc.vector)
+        scatter(1)
+        nc.sync.dma_start(out, window[:])

@@ -19,6 +19,7 @@ MULT = mybir.AluOpType.mult
 ADD = mybir.AluOpType.add
 MIN = mybir.AluOpType.min
 X = mybir.AxisListType.X
+H = T // 2
 
 
 def tile_attend_x_router_ks_kernel(tc, xq, kT, vT, ks, vs, offs, qoffs, out):
@@ -26,22 +27,17 @@ def tile_attend_x_router_ks_kernel(tc, xq, kT, vT, ks, vs, offs, qoffs, out):
     with ExitStack() as ctx:
         lists = ctx.enter_context(tc.tile_pool(name="lists", bufs=1))
         keep = ctx.enter_context(tc.tile_pool(name="keep", bufs=1))
-        ring = ctx.enter_context(tc.tile_pool(name="ring", bufs=2))
         banks = ctx.enter_context(tc.psum_pool(name="banks", bufs=1))
 
         slots = lists.tile([P, N // 16], U16, name="slots")
-        nc.sync.dma_start(slots[:], offs)
         qlist = lists.tile([P, NQ // 16], U16, name="qlist")
-        nc.sync.dma_start(qlist[:], qoffs)
-
         ksw = keep.tile([P, T], F32, name="ksw")
         vsw = keep.tile([P, T], F32, name="vsw")
+        nc.vector.memset(ksw[:], 0.0)
         warm = keep.tile([P, 1], F32, name="warm")
         nc.vector.memset(warm[:], 0.0)
-        nc.vector.memset(ksw[:], 0.0)
-        nc.gpsimd.memset(vsw[:], 0.0)
+        nc.vector.memset(vsw[:], 0.0)
         nc.scalar.activation(warm[:], warm[:], EXP)
-
         ident = keep.tile([P, P], F32, name="ident")
         make_identity(nc, ident[:])
         ident_bf16 = keep.tile([P, P], BF16, name="ident_bf16")
@@ -49,16 +45,25 @@ def tile_attend_x_router_ks_kernel(tc, xq, kT, vT, ks, vs, offs, qoffs, out):
 
         kview = kT.rearrange("(p t) w -> p t w", t=4)
         qview = xq.rearrange("(p t) w -> p t w", t=4)
-        H = T // 2
         raw = {}
-        for key, view, e in (("k0", kview, 0), ("k1", kview, 1), ("q0", qview, 0)):
-            r = keep.tile([P, 2, T], F32, name="raw_" + key)
-            for lo, hi in ((0, 512), (512, H), (H, T)) if key == "k0" else ((0, H), (H, T)):
-                nc.sync.dma_start(r[:, :, lo:hi], view[:, 2 * e : 2 * e + 2, lo:hi])
-                if key == "k0" and lo < H:
-                    scale_window, scale_input = (ksw, ks) if lo == 0 else (vsw, vs)
-                    nc.sync.dma_start(scale_window[0:1, :], scale_input[0:1, :])
-            raw[key] = r
+        for key in ("k0", "k1", "q0"):
+            raw_tile = keep.tile([P, 2, T], F32, name="raw_" + key)
+            raw[key] = raw_tile
+
+        def load_pair(key, view, e, lo, hi):
+            nc.sync.dma_start(raw[key][:, :, lo:hi], view[:, 2 * e : 2 * e + 2, lo:hi])
+
+        load_pair("k0", kview, 0, 0, 768)
+        nc.sync.dma_start(slots[:], offs)
+        nc.sync.dma_start(qlist[:], qoffs)
+        load_pair("k0", kview, 0, 768, H)
+        nc.sync.dma_start(ksw[0:1, :], ks[0:1, :])
+        load_pair("k0", kview, 0, H, T)
+        nc.sync.dma_start(vsw[0:1, :], vs[0:1, :])
+        for lo, hi in ((0, H), (H, T)):
+            load_pair("k1", kview, 1, lo, hi)
+        for lo, hi in ((0, H), (H, T)):
+            load_pair("q0", qview, 0, lo, hi)
         qpl = {}
         for t in (2, 3):
             q_t = keep.tile([P, T], F32, name="qplane%d" % t)
@@ -68,39 +73,34 @@ def tile_attend_x_router_ks_kernel(tc, xq, kT, vT, ks, vs, offs, qoffs, out):
         nc.sync.dma_start(vraw[:], vT)
 
         window = keep.tile([P, T], F32, name="window")
-        nc.gpsimd.memset(window[:], 0.0)
+        for i in range(8):
+            nc.gpsimd.memset(window[:, i * 256 : (i + 1) * 256], 0.0)
 
         ksg = keep.tile([P, N], F32, name="ksg")
         nc.vector.tensor_copy(ksg[:], ksw[:].indirect(slots[:]))
         vsg = keep.tile([P, N], F32, name="vsg")
         nc.vector.tensor_copy(vsg[:], vsw[:].indirect(slots[:]))
-        def to_column(name, gathered, factor):
-            col = keep.tile([P, 8], F32, name=name + "_col")
-            for g in range(2):
-                b = banks.tile([P, 4, P], F32, name="%s_b%d" % (name, g), tag="t", bufs=3)
-                for i in range(4):
-                    nc.tensor.transpose(b[:, i, :], gathered[:, (4 * g + i) * P : (4 * g + i + 1) * P], ident[:])
-                nc.vector.tensor_scalar(col[:, 4 * g : 4 * g + 4], b[:, :, 0], factor, None, MULT)
-            return col
 
-        def to_rows(name, col):
-            row = keep.tile([P, N], F32, name=name + "_row")
-            for g in range(2):
-                b = banks.tile([P, 4 * P], F32, name="%s_r%d" % (name, g), tag="t", bufs=3)
-                for i in range(4):
-                    c = 4 * g + i
-                    nc.tensor.transpose(b[:, i * P : (i + 1) * P], col[:, c : c + 1].to_broadcast([P, P]), ident[:])
-                nc.scalar.copy(row[:, g * 512 : (g + 1) * 512], b[:])
-            return row
-
-        nks_col = to_column("nks", ksg, -1.0)
-        vs_col = to_column("vs", vsg, 1.0)
+        nks_col = keep.tile([P, 8], F32, name="nks_col")
+        vs_col = keep.tile([P, 8], F32, name="vs_col")
+        for g in range(2):
+            b = banks.tile([P, 4, P], F32, name="ksb%d" % g, tag="t", bufs=4)
+            for i in range(4):
+                nc.tensor.transpose(b[:, i, :], ksg[:, (4 * g + i) * P : (4 * g + i + 1) * P], ident[:])
+            nc.vector.tensor_scalar(nks_col[:, 4 * g : 4 * g + 4], b[:, :, 0], -1.0, None, MULT)
+        for g in range(2):
+            b = banks.tile([P, 4, P], F32, name="vsb%d" % g, tag="t", bufs=4)
+            for t in range(4):
+                nc.tensor.transpose(b[:, t, :], vsg[:, g * 512 + t : (g + 1) * 512 : 4], ident[:])
+            nc.vector.tensor_copy(vs_col[:, 4 * g : 4 * g + 4], b[:, :, 0])
 
         kx = keep.tile([P, 4 * N], BF16, name="kx", align_bytes=64)
         qx = keep.tile([P, 4 * NQ], BF16, name="qx", align_bytes=64)
         pair = {}
 
         def cast(key, lo, hi, engine):
+            if lo == hi:
+                return
             dst = pair[key][:].rearrange("p (w e) -> p w e", e=2)[:, lo:hi, :]
             src = raw[key][:, :, lo:hi].rearrange("p e w -> p w e")
             if engine == "s":
@@ -115,23 +115,30 @@ def tile_attend_x_router_ks_kernel(tc, xq, kT, vT, ks, vs, offs, qoffs, out):
         for key in ("k0", "k1", "q0"):
             pair_tile = keep.tile([P, 2 * T], BF16, name="pair_" + key, align_bytes=64)
             pair[key] = pair_tile
-        cast("k0", 0, 512, "s")
-        cast("k0", 512, H, "s")
+        cast("k0", 0, 768, "s")
+        cast("k0", 768, H, "s")
         cast("k0", H, T, "s")
         gather_pair("k0", kx, 0, slots[:])
         cast("k1", 0, H, "s")
-        cast("k1", H, H + H // 2, "s")
-        cast("k1", H + H // 2, T, "v")
+        cast("k1", H, 1536, "s")
+        cast("k1", 1536, T, "v")
         gather_pair("k1", kx, 1, slots[:])
         kc = keep.tile([P, N], U32, name="kc", align_bytes=64)
         ksc = keep.tile([P, N], U8, name="ksc", align_bytes=64)
         nc.vector.quantize_mx(out=kc[:].bitcast(FP8X4), scales=ksc[:], in_=kx[:])
         cast("q0", 0, H, "s")
-        cast("q0", H, H + H // 2, "s")
-        cast("q0", H + H // 2, T, "v")
+        cast("q0", H, 1536, "s")
+        cast("q0", 1536, T, "v")
         gather_pair("q0", qx, 0, qlist[:])
-        nks_row = to_rows("nks", nks_col)
-        vs_row = to_rows("vs", vs_col)
+
+        nks_row = keep.tile([P, 2, 4, P], F32, name="nks_row")
+        for g in range(2):
+            b = banks.tile([P, 4 * P], F32, name="ksr%d" % g, tag="t", bufs=4)
+            for i in range(4):
+                c = 4 * g + i
+                nc.tensor.transpose(b[:, i * P : (i + 1) * P], nks_col[:, c : c + 1].to_broadcast([P, P]), ident[:])
+            nc.scalar.copy(nks_row[:, g, :, :], b[:].rearrange("p (s t) -> p t s", t=4))
+
         qc = keep.tile([P, NQ], U32, name="qc", align_bytes=64)
         qsc = keep.tile([P, NQ], U8, name="qsc", align_bytes=64)
 
@@ -141,7 +148,7 @@ def tile_attend_x_router_ks_kernel(tc, xq, kT, vT, ks, vs, offs, qoffs, out):
 
         gather_q(2, 0, 512)
         for h in range(2):
-            gather_q(3, h * 256, (h + 1) * 256)
+            gather_q(3, h * 224, (h + 1) * 256)
             nc.vector.quantize_mx(
                 out=qc[:, h * 256 : (h + 1) * 256].bitcast(FP8X4),
                 scales=qsc[:, h * 256 : (h + 1) * 256],
@@ -149,8 +156,15 @@ def tile_attend_x_router_ks_kernel(tc, xq, kT, vT, ks, vs, offs, qoffs, out):
             )
 
         nm = keep.tile([P, 4], F32, name="nm")
-        lparts = keep.tile([P, 4, 2], F32, name="lparts")
+        total = keep.tile([P, 4], F32, name="total")
+        y_sb = keep.tile([P, NQ], F32, name="y_sb")
+        rl_sb = keep.tile([P, NQ], F32, name="rl_sb")
+        rl = keep.tile([P, 4], F32, name="rl")
+        BY_SLOT = (2, 3)
+        C0 = min(BY_SLOT) if BY_SLOT else 4
+        found = {}
         state = {}
+        ybanks = []
 
         def scores(j):
             q_cols = slice(j * P, (j + 1) * P)
@@ -168,62 +182,120 @@ def tile_attend_x_router_ks_kernel(tc, xq, kT, vT, ks, vs, offs, qoffs, out):
                     stop=True,
                 )
                 res.append(b)
-            state[j] = res
+            found[j] = res
+
+        at = keep.tile([P, 8, 2 * P], F32, name="at")
+
+        def scores_by_slot():
+            width = (4 - C0) * P
+            q_cols = slice(C0 * P, NQ)
+            per = 512 // width
+            for half in range(8 // per):
+                b = banks.tile([P, 512], F32, name="ss%d" % half, tag="s", bufs=4)
+                for i in range(per):
+                    k_cols = slice((per * half + i) * P, (per * half + i + 1) * P)
+                    nc.tensor.matmul_mx(
+                        out=b[:, i * width : (i + 1) * width],
+                        lhsT=kc[:, k_cols].bitcast(FP8X4),
+                        lhsT_scale=ksc[:, k_cols],
+                        rhs=qc[:, q_cols].bitcast(FP8X4),
+                        rhs_scale=qsc[:, q_cols],
+                        start=True,
+                        stop=True,
+                    )
+                for i in range(per):
+                    c = per * half + i
+                    nc.scalar.activation(
+                        at[:, c, 0:width], b[:, i * width : (i + 1) * width], COPY, scale=nks_col[:, c : c + 1]
+                    )
 
         def scale_rows(j):
-            a = ring.tile([P, N], F32, name="a%d" % j, tag="a")
-            for g in range(2):
-                half = slice(g * 512, (g + 1) * 512)
-                nc.vector.tensor_tensor(a[:, half], state[j][g][:], nks_row[:, half], MULT)
-            nc.vector.tensor_reduce(nm[:, j : j + 1], a[:], X, MIN)
-            state[j] = [a[:, g * 512 : (g + 1) * 512] for g in range(2)]
+            if j in BY_SLOT:
+                res = []
+                for g in range(2):
+                    b = banks.tile([P, 512], F32, name="ts%d_%d" % (j, g), tag="s", bufs=4)
+                    for i in range(4):
+                        nc.tensor.transpose(
+                            b[:, i * P : (i + 1) * P], at[:, 4 * g + i, (j - C0) * P : (j - C0 + 1) * P], ident[:]
+                        )
+                    res.append(b)
+                found[j] = res
+            else:
+                a = keep.tile([P, 2, 4, P], F32, name="a%d" % j)
+                for g in range(2):
+                    nc.vector.tensor_tensor(
+                        a[:, g, :, :], found[j][g][:].rearrange("p (s t) -> p t s", t=4), nks_row[:, g, :, :], MULT
+                    )
+                found[j] = a
+            p = keep.tile([P, 2, 4, P], F32, name="p%d" % j)
+            wx = keep.tile([P, 2, 4 * P], BF16, name="wx%d" % j, align_bytes=64)
+            wc = keep.tile([P, 2 * P], U32, name="wc%d" % j, align_bytes=64)
+            wsc = keep.tile([P, 2 * P], U8, name="wsc%d" % j, align_bytes=64)
+            state[j] = (p, wx, wc, wsc)
+
+        def stabiliser(j):
+            if j in BY_SLOT:
+                half = keep.tile([P, 2], F32, name="half%d" % j)
+                for g in range(2):
+                    nc.vector.tensor_reduce(half[:, g : g + 1], found[j][g][:], X, MIN)
+                nc.vector.tensor_tensor(nm[:, j : j + 1], half[:, 0:1], half[:, 1:2], MIN)
+            else:
+                nc.vector.tensor_reduce(nm[:, j : j + 1], found[j][:].rearrange("p g t s -> p (g t s)"), X, MIN)
 
         def weights(j):
-            p = ring.tile([P, N], F32, name="p%d" % j, tag="p")
-            for g in range(2):
+            p = state[j][0]
+            if (1, 1, 1, 2)[j] == 1 and j not in BY_SLOT:
                 nc.scalar.activation(
-                    p[:, g * 512 : (g + 1) * 512],
-                    state[j][g],
+                    p[:].rearrange("p g t s -> p (g t s)"),
+                    found[j][:].rearrange("p g t s -> p (g t s)"),
                     EXP,
                     bias=nm[:, j : j + 1],
                     scale=-1.0,
-                    accum_out=lparts[:, j, g : g + 1],
+                    accum_out=total[:, j : j + 1],
                 )
-            state[j] = p
+                return
+            parts = keep.tile([P, 2], F32, name="parts%d" % j)
+            for g in range(2):
+                src = found[j][g][:].rearrange("p (s t) -> p t s", t=4) if j in BY_SLOT else found[j][:, g, :, :]
+                nc.scalar.activation(
+                    p[:, g, :, :], src, EXP, bias=nm[:, j : j + 1], scale=-1.0, accum_out=parts[:, g : g + 1]
+                )
+            nc.gpsimd.tensor_tensor(total[:, j : j + 1], parts[:, 0:1], parts[:, 1:2], ADD)
 
-        def start_weights(j):
-            w = ring.tile([P, N], BF16, name="w%d" % j, tag="w")
-            wx = ring.tile([P, 2, 4 * P], BF16, name="wx%d" % j, tag="wx", align_bytes=64)
-            wc = ring.tile([P, 2 * P], U32, name="wc%d" % j, tag="wc", align_bytes=64)
-            wsc = ring.tile([P, 2 * P], U8, name="wsc%d" % j, tag="wsc", align_bytes=64)
-            state[j] = (state[j], w, wx, wc, wsc)
+        def turn_and_scale(j):
+            p, wx, wc, wsc = state[j]
+            for g in range(2):
+                b = banks.tile([P, 4, P], F32, name="pt%d_%d" % (j, g), tag="t", bufs=4)
+                for t in range(4):
+                    nc.tensor.transpose(b[:, t, :], p[:, g, t, :], ident[:])
+                nc.vector.tensor_tensor(
+                    wx[:, g, :].rearrange("p (q t) -> p q t", t=4),
+                    b[:].rearrange("p t q -> p q t"),
+                    vs_col[:, 4 * g : 4 * g + 4].unsqueeze(1).to_broadcast([P, P, 4]),
+                    MULT,
+                )
 
-        def scale_weights(j, g, engine):
-            p, w, wx, wc, wsc = state[j]
-            half = slice(g * 512, (g + 1) * 512)
-            engine.tensor_tensor(w[:, half], p[:, half], vs_row[:, half], MULT)
-
-        def turn_weights(j, g, copy):
-            p, w, wx, wc, wsc = state[j]
-            words = w[:, g * 512 : (g + 1) * 512].bitcast(F32)
-            b = banks.tile([P, 2, P], F32, name="pt%d_%d" % (j, g), tag="t", bufs=3)
-            for u in range(2):
-                nc.tensor.transpose(b[:, u, :], words[:, u::2], ident[:])
-            copy(wx[:, g, :].bitcast(F32).rearrange("p (q u) -> p q u", u=2), b[:].rearrange("p u q -> p q u"))
-
-        def quantise_weights(j, g):
-            p, w, wx, wc, wsc = state[j]
-            cols = slice(g * P, (g + 1) * P)
-            nc.vector.quantize_mx(out=wc[:, cols].bitcast(FP8X4), scales=wsc[:, cols], in_=wx[:, g, :])
-
-        ybank = banks.tile([P, NQ], F32, name="ybank", tag="y", bufs=1)
+        def quantise_weights(j):
+            p, wx, wc, wsc = state[j]
+            cuts = (1, 1, 1, 2)[j]
+            gs = 2 // cuts
+            for i in range(cuts):
+                cols = slice(i * gs * P, (i + 1) * gs * P)
+                nc.vector.quantize_mx(
+                    out=wc[:, cols].bitcast(FP8X4),
+                    scales=wsc[:, cols],
+                    in_=wx[:, i * gs : (i + 1) * gs, :].rearrange("p g n -> p (g n)"),
+                )
 
         def values(j):
-            p, w, wx, wc, wsc = state[j]
+            p, wx, wc, wsc = state[j]
+            if j % 2 == 0:
+                y_bank = banks.tile([P, 2 * P], F32, name="y%d" % j, tag="s", bufs=4)
+                ybanks.append(y_bank)
             for g in range(2):
                 cols = slice(g * P, (g + 1) * P)
                 nc.tensor.matmul_mx(
-                    out=ybank[:, j * P : (j + 1) * P],
+                    out=ybanks[j // 2][:, j % 2 * P : (j % 2 + 1) * P],
                     lhsT=vc[:, cols].bitcast(FP8X4),
                     lhsT_scale=vsc[:, cols],
                     rhs=wc[:, cols].bitcast(FP8X4),
@@ -232,70 +304,76 @@ def tile_attend_x_router_ks_kernel(tc, xq, kT, vT, ks, vs, offs, qoffs, out):
                     stop=(g == 1),
                 )
 
-        y_sb = keep.tile([P, NQ], F32, name="y_sb")
-        rl_sb = keep.tile([P, NQ], F32, name="rl_sb")
-        rl = keep.tile([P, 4], F32, name="rl")
-        lsum = keep.tile([P, 4], F32, name="lsum")
-
-        def scatter(h):
+        def normaliser(h):
             js = slice(2 * h, 2 * h + 2)
-            nc.gpsimd.tensor_tensor(lsum[:, js], lparts[:, js, 0], lparts[:, js, 1], ADD)
-            nc.vector.reciprocal(rl[:, js], lsum[:, js])
-            b = banks.tile([P, 256], F32, name="rlb%d" % h, tag="t", bufs=3)
+            nc.vector.reciprocal(rl[:, js], total[:, js])
+            b = banks.tile([P, 256], F32, name="rlb%d" % h, tag="t", bufs=4)
             for i in range(2):
                 c = 2 * h + i
                 nc.tensor.transpose(b[:, i * P : (i + 1) * P], rl[:, c : c + 1].to_broadcast([P, P]), ident[:])
+            nc.scalar.copy(rl_sb[:, h * 256 : (h + 1) * 256], b[:])
+
+        def scatter(h):
             cols = slice(h * 256, (h + 1) * 256)
-            nc.scalar.copy(rl_sb[:, cols], b[:])
-            nc.scalar.copy(y_sb[:, cols], ybank[:, cols])
+            nc.scalar.copy(y_sb[:, cols], ybanks[h][:])
             nc.vector.tensor_tensor(
                 window[:].indirect(qlist[:, h * 16 : (h + 1) * 16]), y_sb[:, cols], rl_sb[:, cols], MULT
             )
 
-        for j in range(4):
-            scores(j)
-
         vb = keep.tile([P, T], BF16, name="vb")
-        for i in range(4):
-            nc.scalar.activation(vb[:, i * 512 : (i + 1) * 512], vraw[:, i * 512 : (i + 1) * 512], COPY)
         vg = keep.tile([P, N, 2], BF16, name="vg")
-        for g in range(2):
-            nc.scalar.activation(
-                vg[:, g * 512 : (g + 1) * 512, 0], vb[:].indirect(slots[:, g * 32 : (g + 1) * 32]), COPY
-            )
         vx = keep.tile([P, 2, DV, 4], BF16, name="vx", align_bytes=64)
-        for g in range(2):
-            b = banks.tile([P, 4, DV], BF16, name="vt%d" % g, tag="t", bufs=3)
-            for t in range(4):
-                nc.tensor.transpose(b[:, t, :], vg[:, g * 512 + t : (g + 1) * 512 : 4, 0], ident_bf16[:])
-            nc.scalar.copy(vx[:, g, :, :], b[:].rearrange("p t e -> p e t"))
         vc = keep.tile([P, 2 * DV], U32, name="vc", align_bytes=64)
         vsc = keep.tile([P, 2 * DV], U8, name="vsc", align_bytes=64)
 
-        def finish(j, engine):
-            start_weights(j)
-            for g in range(2):
-                scale_weights(j, g, engine)
-                turn_weights(j, g, nc.scalar.copy)
-                quantise_weights(j, g)
-            if j == 0:
-                nc.vector.quantize_mx(
-                    out=vc[:].bitcast(FP8X4), scales=vsc[:], in_=vx[:].rearrange("p g e t -> p (g e t)")
-                )
-            values(j)
+        def load_values():
+            for i in range(2):
+                cols = slice(i * H, (i + 1) * H)
+                nc.scalar.activation(vb[:, cols], vraw[:, cols], COPY)
 
+        def gather_values():
+            for g in range(2):
+                nc.scalar.activation(
+                    vg[:, g * 512 : (g + 1) * 512, 0], vb[:].indirect(slots[:, g * 32 : (g + 1) * 32]), COPY
+                )
+            for g in range(2):
+                b = banks.tile([P, 4, DV], BF16, name="vt%d" % g, tag="t", bufs=4)
+                for t in range(4):
+                    nc.tensor.transpose(b[:, t, :], vg[:, g * 512 + t : (g + 1) * 512 : 4, 0], ident_bf16[:])
+                nc.scalar.copy(vx[:, g, :, :], b[:].rearrange("p t e -> p e t"))
+
+        scores(0)
+        scores(1)
+        scores_by_slot()
         scale_rows(0)
-        weights(0)
-        scale_rows(1)
-        weights(1)
-        finish(0, nc.gpsimd)
-        scale_rows(2)
-        weights(2)
-        finish(1, nc.gpsimd)
         scale_rows(3)
+        stabiliser(0)
+        scale_rows(2)
+        stabiliser(2)
+        weights(0)
+        weights(2)
+        load_values()
+        scale_rows(1)
+        stabiliser(1)
+        turn_and_scale(0)
+        stabiliser(3)
+        weights(1)
+        gather_values()
+        quantise_weights(0)
+        turn_and_scale(1)
+        nc.vector.quantize_mx(out=vc[:].bitcast(FP8X4), scales=vsc[:], in_=vx[:].rearrange("p g e t -> p (g e t)"))
+        values(0)
         weights(3)
+        quantise_weights(1)
+        turn_and_scale(2)
+        quantise_weights(2)
+        normaliser(0)
+        turn_and_scale(3)
+        values(1)
+        normaliser(1)
+        quantise_weights(3)
+        values(2)
+        values(3)
         scatter(0)
-        finish(2, nc.gpsimd)
-        finish(3, nc.vector)
         scatter(1)
         nc.sync.dma_start(out, window[:])

@@ -33,10 +33,12 @@ def tile_attend_x_router_ks_kernel(tc, xq, kT, vT, ks, vs, offs, qoffs, out):
         qlist = lists.tile([P, NQ // 16], U16, name="qlist")
         ksw = keep.tile([P, T], F32, name="ksw")
         vsw = keep.tile([P, T], F32, name="vsw")
-        nc.vector.memset(ksw[:], 0.0)
         warm = keep.tile([P, 1], F32, name="warm")
+        nc.vector.memset(ksw[:, 0:H], 0.0)
+        nc.gpsimd.memset(ksw[:, H:T], 0.0)
         nc.vector.memset(warm[:], 0.0)
-        nc.vector.memset(vsw[:], 0.0)
+        nc.vector.memset(vsw[:, 0:H], 0.0)
+        nc.gpsimd.memset(vsw[:, H:T], 0.0)
         nc.scalar.activation(warm[:], warm[:], EXP)
         ident = keep.tile([P, P], F32, name="ident")
         make_identity(nc, ident[:])
@@ -56,8 +58,8 @@ def tile_attend_x_router_ks_kernel(tc, xq, kT, vT, ks, vs, offs, qoffs, out):
         load_pair("k0", kview, 0, 0, 768)
         nc.sync.dma_start(slots[:], offs)
         nc.sync.dma_start(qlist[:], qoffs)
-        load_pair("k0", kview, 0, 768, H)
         nc.sync.dma_start(ksw[0:1, :], ks[0:1, :])
+        load_pair("k0", kview, 0, 768, H)
         load_pair("k0", kview, 0, H, T)
         nc.sync.dma_start(vsw[0:1, :], vs[0:1, :])
         for lo, hi in ((0, H), (H, T)):
@@ -69,7 +71,7 @@ def tile_attend_x_router_ks_kernel(tc, xq, kT, vT, ks, vs, offs, qoffs, out):
             q_t = keep.tile([P, T], F32, name="qplane%d" % t)
             nc.sync.dma_start(q_t[:], qview[:, t, :])
             qpl[t] = q_t
-        vraw = keep.tile([P, T], F32, name="vraw")
+        vraw = keep.tile([P, T], F32, name="vraw", tag="vraw")
         nc.sync.dma_start(vraw[:], vT)
 
         window = keep.tile([P, T], F32, name="window")
@@ -84,12 +86,12 @@ def tile_attend_x_router_ks_kernel(tc, xq, kT, vT, ks, vs, offs, qoffs, out):
         nks_col = keep.tile([P, 8], F32, name="nks_col")
         vs_col = keep.tile([P, 8], F32, name="vs_col")
         for g in range(2):
-            b = banks.tile([P, 4, P], F32, name="ksb%d" % g, tag="t", bufs=4)
+            b = banks.tile([P, 4, P], F32, name="ksb%d" % g, tag="b%d" % g, bufs=1)
             for i in range(4):
                 nc.tensor.transpose(b[:, i, :], ksg[:, (4 * g + i) * P : (4 * g + i + 1) * P], ident[:])
             nc.vector.tensor_scalar(nks_col[:, 4 * g : 4 * g + 4], b[:, :, 0], -1.0, None, MULT)
         for g in range(2):
-            b = banks.tile([P, 4, P], F32, name="vsb%d" % g, tag="t", bufs=4)
+            b = banks.tile([P, 4, P], F32, name="vsb%d" % g, tag="b%d" % (2 + g), bufs=1)
             for t in range(4):
                 nc.tensor.transpose(b[:, t, :], vsg[:, g * 512 + t : (g + 1) * 512 : 4], ident[:])
             nc.vector.tensor_copy(vs_col[:, 4 * g : 4 * g + 4], b[:, :, 0])
@@ -117,7 +119,8 @@ def tile_attend_x_router_ks_kernel(tc, xq, kT, vT, ks, vs, offs, qoffs, out):
             pair[key] = pair_tile
         cast("k0", 0, 768, "s")
         cast("k0", 768, H, "s")
-        cast("k0", H, T, "s")
+        cast("k0", H, 1536, "s")
+        cast("k0", 1536, T, "v")
         gather_pair("k0", kx, 0, slots[:])
         cast("k1", 0, H, "s")
         cast("k1", H, 1536, "s")
@@ -127,13 +130,12 @@ def tile_attend_x_router_ks_kernel(tc, xq, kT, vT, ks, vs, offs, qoffs, out):
         ksc = keep.tile([P, N], U8, name="ksc", align_bytes=64)
         nc.vector.quantize_mx(out=kc[:].bitcast(FP8X4), scales=ksc[:], in_=kx[:])
         cast("q0", 0, H, "s")
-        cast("q0", H, 1536, "s")
-        cast("q0", 1536, T, "v")
+        cast("q0", H, T, "s")
         gather_pair("q0", qx, 0, qlist[:])
 
         nks_row = keep.tile([P, 2, 4, P], F32, name="nks_row")
         for g in range(2):
-            b = banks.tile([P, 4 * P], F32, name="ksr%d" % g, tag="t", bufs=4)
+            b = banks.tile([P, 4 * P], F32, name="ksr%d" % g, tag="b%d" % (4 + g), bufs=1)
             for i in range(4):
                 c = 4 * g + i
                 nc.tensor.transpose(b[:, i * P : (i + 1) * P], nks_col[:, c : c + 1].to_broadcast([P, P]), ident[:])
@@ -160,8 +162,9 @@ def tile_attend_x_router_ks_kernel(tc, xq, kT, vT, ks, vs, offs, qoffs, out):
         y_sb = keep.tile([P, NQ], F32, name="y_sb")
         rl_sb = keep.tile([P, NQ], F32, name="rl_sb")
         rl = keep.tile([P, 4], F32, name="rl")
-        BY_SLOT = (2, 3)
-        C0 = min(BY_SLOT) if BY_SLOT else 4
+        R = (0, 1)
+        by_slot = {}
+        SB, TB, PB, VB, YB, RB = ({0: (0, 1), 1: (2, 3), 2: (4, 5, 6, 7)}, {2: (0, 1), 3: (2, 3)}, {0: (4, 5), 1: (7, 4), 2: (5, 0), 3: (1, 2)}, 6, (6, 7), (3, 3))
         found = {}
         state = {}
         ybanks = []
@@ -170,7 +173,7 @@ def tile_attend_x_router_ks_kernel(tc, xq, kT, vT, ks, vs, offs, qoffs, out):
             q_cols = slice(j * P, (j + 1) * P)
             res = []
             for g in range(2):
-                b = banks.tile([P, 512], F32, name="sc%d_%d" % (j, g), tag="s", bufs=4)
+                b = banks.tile([P, 512], F32, name="sc%d_%d" % (j, g), tag="b%d" % SB[j][g], bufs=1)
                 k_cols = slice(g * 512, (g + 1) * 512)
                 nc.tensor.matmul_mx(
                     out=b[:],
@@ -184,16 +187,15 @@ def tile_attend_x_router_ks_kernel(tc, xq, kT, vT, ks, vs, offs, qoffs, out):
                 res.append(b)
             found[j] = res
 
-        at = keep.tile([P, 8, 2 * P], F32, name="at")
-
-        def scores_by_slot():
-            width = (4 - C0) * P
-            q_cols = slice(C0 * P, NQ)
+        def scores_by_slot(js):
+            width = len(js) * P
+            q_cols = slice(js[0] * P, (js[-1] + 1) * P)
             per = 512 // width
-            for half in range(8 // per):
-                b = banks.tile([P, 512], F32, name="ss%d" % half, tag="s", bufs=4)
+            at = keep.tile([P, 8, width], F32, name="at%d" % js[0], tag="vraw")
+            for n in range(8 // per):
+                b = banks.tile([P, 512], F32, name="ss%d_%d" % (js[0], n), tag="b%d" % SB[js[0]][n], bufs=1)
                 for i in range(per):
-                    k_cols = slice((per * half + i) * P, (per * half + i + 1) * P)
+                    k_cols = slice((per * n + i) * P, (per * n + i + 1) * P)
                     nc.tensor.matmul_mx(
                         out=b[:, i * width : (i + 1) * width],
                         lhsT=kc[:, k_cols].bitcast(FP8X4),
@@ -204,19 +206,22 @@ def tile_attend_x_router_ks_kernel(tc, xq, kT, vT, ks, vs, offs, qoffs, out):
                         stop=True,
                     )
                 for i in range(per):
-                    c = per * half + i
+                    c = per * n + i
                     nc.scalar.activation(
-                        at[:, c, 0:width], b[:, i * width : (i + 1) * width], COPY, scale=nks_col[:, c : c + 1]
+                        at[:, c, :], b[:, i * width : (i + 1) * width], COPY, scale=nks_col[:, c : c + 1]
                     )
+            for i, j in enumerate(js):
+                by_slot[j] = (at, i)
 
         def scale_rows(j):
-            if j in BY_SLOT:
+            if j not in R:
+                at, col = by_slot[j]
                 res = []
                 for g in range(2):
-                    b = banks.tile([P, 512], F32, name="ts%d_%d" % (j, g), tag="s", bufs=4)
+                    b = banks.tile([P, 512], F32, name="ts%d_%d" % (j, g), tag="b%d" % TB[j][g], bufs=1)
                     for i in range(4):
                         nc.tensor.transpose(
-                            b[:, i * P : (i + 1) * P], at[:, 4 * g + i, (j - C0) * P : (j - C0 + 1) * P], ident[:]
+                            b[:, i * P : (i + 1) * P], at[:, 4 * g + i, col * P : (col + 1) * P], ident[:]
                         )
                     res.append(b)
                 found[j] = res
@@ -234,7 +239,7 @@ def tile_attend_x_router_ks_kernel(tc, xq, kT, vT, ks, vs, offs, qoffs, out):
             state[j] = (p, wx, wc, wsc)
 
         def stabiliser(j):
-            if j in BY_SLOT:
+            if j not in R:
                 half = keep.tile([P, 2], F32, name="half%d" % j)
                 for g in range(2):
                     nc.vector.tensor_reduce(half[:, g : g + 1], found[j][g][:], X, MIN)
@@ -244,7 +249,7 @@ def tile_attend_x_router_ks_kernel(tc, xq, kT, vT, ks, vs, offs, qoffs, out):
 
         def weights(j):
             p = state[j][0]
-            if (1, 1, 1, 2)[j] == 1 and j not in BY_SLOT:
+            if j in R:
                 nc.scalar.activation(
                     p[:].rearrange("p g t s -> p (g t s)"),
                     found[j][:].rearrange("p g t s -> p (g t s)"),
@@ -256,7 +261,7 @@ def tile_attend_x_router_ks_kernel(tc, xq, kT, vT, ks, vs, offs, qoffs, out):
                 return
             parts = keep.tile([P, 2], F32, name="parts%d" % j)
             for g in range(2):
-                src = found[j][g][:].rearrange("p (s t) -> p t s", t=4) if j in BY_SLOT else found[j][:, g, :, :]
+                src = found[j][g][:].rearrange("p (s t) -> p t s", t=4) if j not in R else found[j][:, g, :, :]
                 nc.scalar.activation(
                     p[:, g, :, :], src, EXP, bias=nm[:, j : j + 1], scale=-1.0, accum_out=parts[:, g : g + 1]
                 )
@@ -265,7 +270,7 @@ def tile_attend_x_router_ks_kernel(tc, xq, kT, vT, ks, vs, offs, qoffs, out):
         def turn_and_scale(j):
             p, wx, wc, wsc = state[j]
             for g in range(2):
-                b = banks.tile([P, 4, P], F32, name="pt%d_%d" % (j, g), tag="t", bufs=4)
+                b = banks.tile([P, 4, P], F32, name="pt%d_%d" % (j, g), tag="b%d" % PB[j][g], bufs=1)
                 for t in range(4):
                     nc.tensor.transpose(b[:, t, :], p[:, g, t, :], ident[:])
                 nc.vector.tensor_tensor(
@@ -277,7 +282,7 @@ def tile_attend_x_router_ks_kernel(tc, xq, kT, vT, ks, vs, offs, qoffs, out):
 
         def quantise_weights(j):
             p, wx, wc, wsc = state[j]
-            cuts = (1, 1, 1, 2)[j]
+            cuts = 2 if j == 3 else 1
             gs = 2 // cuts
             for i in range(cuts):
                 cols = slice(i * gs * P, (i + 1) * gs * P)
@@ -290,7 +295,7 @@ def tile_attend_x_router_ks_kernel(tc, xq, kT, vT, ks, vs, offs, qoffs, out):
         def values(j):
             p, wx, wc, wsc = state[j]
             if j % 2 == 0:
-                y_bank = banks.tile([P, 2 * P], F32, name="y%d" % j, tag="s", bufs=4)
+                y_bank = banks.tile([P, 2 * P], F32, name="y%d" % j, tag="b%d" % YB[j // 2], bufs=1)
                 ybanks.append(y_bank)
             for g in range(2):
                 cols = slice(g * P, (g + 1) * P)
@@ -307,7 +312,7 @@ def tile_attend_x_router_ks_kernel(tc, xq, kT, vT, ks, vs, offs, qoffs, out):
         def normaliser(h):
             js = slice(2 * h, 2 * h + 2)
             nc.vector.reciprocal(rl[:, js], total[:, js])
-            b = banks.tile([P, 256], F32, name="rlb%d" % h, tag="t", bufs=4)
+            b = banks.tile([P, 256], F32, name="rlb%d" % h, tag="b%d" % RB[h], bufs=1)
             for i in range(2):
                 c = 2 * h + i
                 nc.tensor.transpose(b[:, i * P : (i + 1) * P], rl[:, c : c + 1].to_broadcast([P, P]), ident[:])
@@ -336,44 +341,44 @@ def tile_attend_x_router_ks_kernel(tc, xq, kT, vT, ks, vs, offs, qoffs, out):
                 nc.scalar.activation(
                     vg[:, g * 512 : (g + 1) * 512, 0], vb[:].indirect(slots[:, g * 32 : (g + 1) * 32]), COPY
                 )
+            b = banks.tile([P, 2, 4, DV], BF16, name="vt", tag="b%d" % VB, bufs=1)
             for g in range(2):
-                b = banks.tile([P, 4, DV], BF16, name="vt%d" % g, tag="t", bufs=4)
                 for t in range(4):
-                    nc.tensor.transpose(b[:, t, :], vg[:, g * 512 + t : (g + 1) * 512 : 4, 0], ident_bf16[:])
-                nc.scalar.copy(vx[:, g, :, :], b[:].rearrange("p t e -> p e t"))
+                    nc.tensor.transpose(b[:, g, t, :], vg[:, g * 512 + t : (g + 1) * 512 : 4, 0], ident_bf16[:])
+            nc.scalar.copy(vx[:], b[:].rearrange("p g t e -> p g e t"))
 
         scores(0)
         scores(1)
-        scores_by_slot()
-        scale_rows(0)
-        scale_rows(3)
-        stabiliser(0)
-        scale_rows(2)
-        stabiliser(2)
-        weights(0)
-        weights(2)
         load_values()
+        scores_by_slot((2, 3,))
+        scale_rows(0)
+        stabiliser(0)
+        weights(0)
         scale_rows(1)
         stabiliser(1)
-        turn_and_scale(0)
-        stabiliser(3)
         weights(1)
         gather_values()
+        scale_rows(2)
+        stabiliser(2)
+        weights(2)
+        scale_rows(3)
+        stabiliser(3)
+        weights(3)
+        turn_and_scale(0)
         quantise_weights(0)
-        turn_and_scale(1)
         nc.vector.quantize_mx(out=vc[:].bitcast(FP8X4), scales=vsc[:], in_=vx[:].rearrange("p g e t -> p (g e t)"))
         values(0)
-        weights(3)
+        turn_and_scale(1)
         quantise_weights(1)
+        values(1)
         turn_and_scale(2)
         quantise_weights(2)
+        values(2)
         normaliser(0)
         turn_and_scale(3)
-        values(1)
         normaliser(1)
-        quantise_weights(3)
-        values(2)
-        values(3)
         scatter(0)
+        quantise_weights(3)
+        values(3)
         scatter(1)
         nc.sync.dma_start(out, window[:])

@@ -34,11 +34,9 @@ def tile_attend_x_router_ks_kernel(tc, xq, kT, vT, ks, vs, offs, qoffs, out):
         ksw = keep.tile([P, T], F32, name="ksw")
         vsw = keep.tile([P, T], F32, name="vsw")
         warm = keep.tile([P, 1], F32, name="warm")
-        nc.vector.memset(ksw[:, 0:H], 0.0)
-        nc.gpsimd.memset(ksw[:, H:T], 0.0)
         nc.vector.memset(warm[:], 0.0)
-        nc.vector.memset(vsw[:, 0:H], 0.0)
-        nc.gpsimd.memset(vsw[:, H:T], 0.0)
+        nc.vector.memset(ksw[:], 0.0)
+        nc.vector.memset(vsw[:], 0.0)
         nc.scalar.activation(warm[:], warm[:], EXP)
         ident = keep.tile([P, P], F32, name="ident")
         make_identity(nc, ident[:])
@@ -55,15 +53,15 @@ def tile_attend_x_router_ks_kernel(tc, xq, kT, vT, ks, vs, offs, qoffs, out):
         def load_pair(key, view, e, lo, hi):
             nc.sync.dma_start(raw[key][:, :, lo:hi], view[:, 2 * e : 2 * e + 2, lo:hi])
 
-        load_pair("k0", kview, 0, 0, 768)
+        load_pair("k0", kview, 0, 0, 512)
         nc.sync.dma_start(slots[:], offs)
         nc.sync.dma_start(qlist[:], qoffs)
+        load_pair("k0", kview, 0, 512, 1280)
         nc.sync.dma_start(ksw[0:1, :], ks[0:1, :])
-        load_pair("k0", kview, 0, 768, H)
-        load_pair("k0", kview, 0, H, T)
+        load_pair("k0", kview, 0, 1280, 2048)
+        load_pair("k1", kview, 1, 0, H)
         nc.sync.dma_start(vsw[0:1, :], vs[0:1, :])
-        for lo, hi in ((0, H), (H, T)):
-            load_pair("k1", kview, 1, lo, hi)
+        load_pair("k1", kview, 1, H, T)
         for lo, hi in ((0, H), (H, T)):
             load_pair("q0", qview, 0, lo, hi)
         qpl = {}
@@ -117,10 +115,10 @@ def tile_attend_x_router_ks_kernel(tc, xq, kT, vT, ks, vs, offs, qoffs, out):
         for key in ("k0", "k1", "q0"):
             pair_tile = keep.tile([P, 2 * T], BF16, name="pair_" + key, align_bytes=64)
             pair[key] = pair_tile
-        cast("k0", 0, 768, "s")
-        cast("k0", 768, H, "s")
-        cast("k0", H, 1536, "s")
-        cast("k0", 1536, T, "v")
+        cast("k0", 0, 512, "s")
+        cast("k0", 512, 1280, "s")
+        cast("k0", 1280, 1536, "s")
+        cast("k0", 1536, 2048, "v")
         gather_pair("k0", kx, 0, slots[:])
         cast("k1", 0, H, "s")
         cast("k1", H, 1536, "s")

from contextlib import ExitStack

import concourse.mybir as mybir
from concourse.masks import make_identity

P = 128
D, T, N, NQ, DV = 512, 2048, 1024, 512, 128
FLOPS = 2 * NQ * N * (D + DV)

F32 = mybir.dt.float32
BF16 = mybir.dt.bfloat16
U32 = mybir.dt.uint32
U16 = mybir.dt.uint16
U8 = mybir.dt.uint8
FP8X4 = mybir.dt.float8_e4m3fn_x4
COPY = mybir.ActivationFunctionType.Copy
EXP = mybir.ActivationFunctionType.Exp
MULT = mybir.AluOpType.mult
ADD = mybir.AluOpType.add
MIN = mybir.AluOpType.min
X = mybir.AxisListType.X
H = T // 2


def tile_attend_x_router_ks_kernel(tc, xq, kT, vT, ks, vs, offs, qoffs, out):
    nc = tc.nc
    with ExitStack() as ctx:
        lists = ctx.enter_context(tc.tile_pool(name="lists", bufs=1))
        keep = ctx.enter_context(tc.tile_pool(name="keep", bufs=1))
        banks = ctx.enter_context(tc.psum_pool(name="banks", bufs=1))

        slots = lists.tile([P, N // 16], U16, name="slots")
        qlist = lists.tile([P, NQ // 16], U16, name="qlist")
        ksw = keep.tile([P, T], F32, name="ksw")
        vsw = keep.tile([P, T], F32, name="vsw")
        warm = keep.tile([P, 1], F32, name="warm")
        nc.vector.memset(warm[:], 0.0)
        nc.vector.memset(ksw[:], 0.0)
        nc.vector.memset(vsw[:], 0.0)
        nc.scalar.activation(warm[:], warm[:], EXP)
        ident = keep.tile([P, P], F32, name="ident")
        make_identity(nc, ident[:])
        ident_bf16 = keep.tile([P, P], BF16, name="ident_bf16")
        make_identity(nc, ident_bf16[:])

        kview = kT.rearrange("(p t) w -> p t w", t=4)
        qview = xq.rearrange("(p t) w -> p t w", t=4)
        raw = {}
        for key in ("k0", "k1", "q0"):
            raw_tile = keep.tile([P, 2, T], F32, name="raw_" + key)
            raw[key] = raw_tile

        def load_pair(key, view, e, lo, hi):
            nc.sync.dma_start(raw[key][:, :, lo:hi], view[:, 2 * e : 2 * e + 2, lo:hi])

        load_pair("k0", kview, 0, 0, 512)
        nc.sync.dma_start(slots[:], offs)
        nc.sync.dma_start(qlist[:], qoffs)
        load_pair("k0", kview, 0, 512, 1280)
        nc.sync.dma_start(ksw[0:1, :], ks[0:1, :])
        load_pair("k0", kview, 0, 1280, 2048)
        load_pair("k1", kview, 1, 0, H)
        nc.sync.dma_start(vsw[0:1, :], vs[0:1, :])
        load_pair("k1", kview, 1, H, T)
        for lo, hi in ((0, H), (H, T)):
            load_pair("q0", qview, 0, lo, hi)
        qpl = {}
        for t in (2, 3):
            q_t = keep.tile([P, T], F32, name="qplane%d" % t)
            nc.sync.dma_start(q_t[:], qview[:, t, :])
            qpl[t] = q_t
        vraw = keep.tile([P, T], F32, name="vraw", tag="vraw")
        nc.sync.dma_start(vraw[:], vT)

        window = keep.tile([P, T], F32, name="window")
        for i in range(8):
            nc.gpsimd.memset(window[:, i * 256 : (i + 1) * 256], 0.0)

        ksg = keep.tile([P, N], F32, name="ksg")
        nc.vector.tensor_copy(ksg[:], ksw[:].indirect(slots[:]))
        vsg = keep.tile([P, N], F32, name="vsg")
        nc.vector.tensor_copy(vsg[:], vsw[:].indirect(slots[:]))

        nks_col = keep.tile([P, 8], F32, name="nks_col")
        vs_col = keep.tile([P, 8], F32, name="vs_col")
        for g in range(2):
            b = banks.tile([P, 4, P], F32, name="ksb%d" % g, tag="b%d" % g, bufs=1)
            for i in range(4):
                nc.tensor.transpose(b[:, i, :], ksg[:, (4 * g + i) * P : (4 * g + i + 1) * P], ident[:])
            nc.vector.tensor_scalar(nks_col[:, 4 * g : 4 * g + 4], b[:, :, 0], -1.0, None, MULT)
        for g in range(2):
            b = banks.tile([P, 4, P], F32, name="vsb%d" % g, tag="b%d" % (2 + g), bufs=1)
            for t in range(4):
                nc.tensor.transpose(b[:, t, :], vsg[:, g * 512 + t : (g + 1) * 512 : 4], ident[:])
            nc.vector.tensor_copy(vs_col[:, 4 * g : 4 * g + 4], b[:, :, 0])

        kx = keep.tile([P, 4 * N], BF16, name="kx", align_bytes=64)
        qx = keep.tile([P, 4 * NQ], BF16, name="qx", align_bytes=64)
        pair = {}

        def cast(key, lo, hi, engine):
            if lo == hi:
                return
            dst = pair[key][:].rearrange("p (w e) -> p w e", e=2)[:, lo:hi, :]
            src = raw[key][:, :, lo:hi].rearrange("p e w -> p w e")
            if engine == "s":
                nc.scalar.activation(dst, src, COPY)
            else:
                nc.vector.tensor_copy(dst, src)

        def gather_pair(key, wide, e, offsets):
            dst = wide[:].bitcast(U32).rearrange("p (n u) -> p n u", u=2)[:, :, e]
            nc.vector.tensor_copy(dst, pair[key][:].bitcast(U32).indirect(offsets))

        for key in ("k0", "k1", "q0"):
            pair_tile = keep.tile([P, 2 * T], BF16, name="pair_" + key, align_bytes=64)
            pair[key] = pair_tile
        cast("k0", 0, 512, "s")
        cast("k0", 512, 1280, "s")
        cast("k0", 1280, 1536, "s")
        cast("k0", 1536, 2048, "v")
        gather_pair("k0", kx, 0, slots[:])
        cast("k1", 0, H, "s")
        cast("k1", H, 1536, "s")
        cast("k1", 1536, T, "v")
        gather_pair("k1", kx, 1, slots[:])
        kc = keep.tile([P, N], U32, name="kc", align_bytes=64)
        ksc = keep.tile([P, N], U8, name="ksc", align_bytes=64)
        nc.vector.quantize_mx(out=kc[:].bitcast(FP8X4), scales=ksc[:], in_=kx[:])
        cast("q0", 0, H, "s")
        cast("q0", H, T, "s")
        gather_pair("q0", qx, 0, qlist[:])

        nks_row = keep.tile([P, 2, 4, P], F32, name="nks_row")
        for g in range(2):
            b = banks.tile([P, 4 * P], F32, name="ksr%d" % g, tag="b%d" % (4 + g), bufs=1)
            for i in range(4):
                c = 4 * g + i
                nc.tensor.transpose(b[:, i * P : (i + 1) * P], nks_col[:, c : c + 1].to_broadcast([P, P]), ident[:])
            nc.scalar.copy(nks_row[:, g, :, :], b[:].rearrange("p (s t) -> p t s", t=4))

        qc = keep.tile([P, NQ], U32, name="qc", align_bytes=64)
        qsc = keep.tile([P, NQ], U8, name="qsc", align_bytes=64)

        def gather_q(t, lo, hi):
            dst = qx[:].rearrange("p (n f) -> p n f", f=4)[:, lo:hi, t]
            nc.vector.tensor_copy(dst, qpl[t][:].indirect(qlist[:, lo // 16 : hi // 16]))

        gather_q(2, 0, 512)
        for h in range(2):
            gather_q(3, h * 224, (h + 1) * 256)
            nc.vector.quantize_mx(
                out=qc[:, h * 256 : (h + 1) * 256].bitcast(FP8X4),
                scales=qsc[:, h * 256 : (h + 1) * 256],
                in_=qx[:, h * 1024 : (h + 1) * 1024],
            )

        nm = keep.tile([P, 4], F32, name="nm")
        total = keep.tile([P, 4], F32, name="total")
        y_sb = keep.tile([P, NQ], F32, name="y_sb")
        rl_sb = keep.tile([P, NQ], F32, name="rl_sb")
        rl = keep.tile([P, 4], F32, name="rl")
        R = (0, 1)
        by_slot = {}
        SB, TB, PB, VB, YB, RB = ({0: (0, 1), 1: (2, 3), 2: (4, 5, 6, 7)}, {2: (0, 1), 3: (2, 3)}, {0: (4, 5), 1: (7, 4), 2: (5, 0), 3: (1, 2)}, 6, (6, 7), (3, 3))
        found = {}
        state = {}
        ybanks = []

        def scores(j):
            q_cols = slice(j * P, (j + 1) * P)
            res = []
            for g in range(2):
                b = banks.tile([P, 512], F32, name="sc%d_%d" % (j, g), tag="b%d" % SB[j][g], bufs=1)
                k_cols = slice(g * 512, (g + 1) * 512)
                nc.tensor.matmul_mx(
                    out=b[:],
                    lhsT=qc[:, q_cols].bitcast(FP8X4),
                    lhsT_scale=qsc[:, q_cols],
                    rhs=kc[:, k_cols].bitcast(FP8X4),
                    rhs_scale=ksc[:, k_cols],
                    start=True,
                    stop=True,
                )
                res.append(b)
            found[j] = res

        def scores_by_slot(js):
            width = len(js) * P
            q_cols = slice(js[0] * P, (js[-1] + 1) * P)
            per = 512 // width
            at = keep.tile([P, 8, width], F32, name="at%d" % js[0], tag="vraw")
            for n in range(8 // per):
                b = banks.tile([P, 512], F32, name="ss%d_%d" % (js[0], n), tag="b%d" % SB[js[0]][n], bufs=1)
                for i in range(per):
                    k_cols = slice((per * n + i) * P, (per * n + i + 1) * P)
                    nc.tensor.matmul_mx(
                        out=b[:, i * width : (i + 1) * width],
                        lhsT=kc[:, k_cols].bitcast(FP8X4),
                        lhsT_scale=ksc[:, k_cols],
                        rhs=qc[:, q_cols].bitcast(FP8X4),
                        rhs_scale=qsc[:, q_cols],
                        start=True,
                        stop=True,
                    )
                for i in range(per):
                    c = per * n + i
                    nc.scalar.activation(
                        at[:, c, :], b[:, i * width : (i + 1) * width], COPY, scale=nks_col[:, c : c + 1]
                    )
            for i, j in enumerate(js):
                by_slot[j] = (at, i)

        def scale_rows(j):
            if j not in R:
                at, col = by_slot[j]
                res = []
                for g in range(2):
                    b = banks.tile([P, 512], F32, name="ts%d_%d" % (j, g), tag="b%d" % TB[j][g], bufs=1)
                    for i in range(4):
                        nc.tensor.transpose(
                            b[:, i * P : (i + 1) * P], at[:, 4 * g + i, col * P : (col + 1) * P], ident[:]
                        )
                    res.append(b)
                found[j] = res
            else:
                a = keep.tile([P, 2, 4, P], F32, name="a%d" % j)
                for g in range(2):
                    nc.vector.tensor_tensor(
                        a[:, g, :, :], found[j][g][:].rearrange("p (s t) -> p t s", t=4), nks_row[:, g, :, :], MULT
                    )
                found[j] = a
            p = keep.tile([P, 2, 4, P], F32, name="p%d" % j)
            wx = keep.tile([P, 2, 4 * P], BF16, name="wx%d" % j, align_bytes=64)
            wc = keep.tile([P, 2 * P], U32, name="wc%d" % j, align_bytes=64)
            wsc = keep.tile([P, 2 * P], U8, name="wsc%d" % j, align_bytes=64)
            state[j] = (p, wx, wc, wsc)

        def stabiliser(j):
            if j not in R:
                half = keep.tile([P, 2], F32, name="half%d" % j)
                for g in range(2):
                    nc.vector.tensor_reduce(half[:, g : g + 1], found[j][g][:], X, MIN)
                nc.vector.tensor_tensor(nm[:, j : j + 1], half[:, 0:1], half[:, 1:2], MIN)
            else:
                nc.vector.tensor_reduce(nm[:, j : j + 1], found[j][:].rearrange("p g t s -> p (g t s)"), X, MIN)

        def weights(j):
            p = state[j][0]
            if j in R:
                nc.scalar.activation(
                    p[:].rearrange("p g t s -> p (g t s)"),
                    found[j][:].rearrange("p g t s -> p (g t s)"),
                    EXP,
                    bias=nm[:, j : j + 1],
                    scale=-1.0,
                    accum_out=total[:, j : j + 1],
                )
                return
            parts = keep.tile([P, 2], F32, name="parts%d" % j)
            for g in range(2):
                src = found[j][g][:].rearrange("p (s t) -> p t s", t=4) if j not in R else found[j][:, g, :, :]
                nc.scalar.activation(
                    p[:, g, :, :], src, EXP, bias=nm[:, j : j + 1], scale=-1.0, accum_out=parts[:, g : g + 1]
                )
            nc.gpsimd.tensor_tensor(total[:, j : j + 1], parts[:, 0:1], parts[:, 1:2], ADD)

        def turn_and_scale(j):
            p, wx, wc, wsc = state[j]
            for g in range(2):
                b = banks.tile([P, 4, P], F32, name="pt%d_%d" % (j, g), tag="b%d" % PB[j][g], bufs=1)
                for t in range(4):
                    nc.tensor.transpose(b[:, t, :], p[:, g, t, :], ident[:])
                nc.vector.tensor_tensor(
                    wx[:, g, :].rearrange("p (q t) -> p q t", t=4),
                    b[:].rearrange("p t q -> p q t"),
                    vs_col[:, 4 * g : 4 * g + 4].unsqueeze(1).to_broadcast([P, P, 4]),
                    MULT,
                )

        def quantise_weights(j):
            p, wx, wc, wsc = state[j]
            cuts = 2 if j == 3 else 1
            gs = 2 // cuts
            for i in range(cuts):
                cols = slice(i * gs * P, (i + 1) * gs * P)
                nc.vector.quantize_mx(
                    out=wc[:, cols].bitcast(FP8X4),
                    scales=wsc[:, cols],
                    in_=wx[:, i * gs : (i + 1) * gs, :].rearrange("p g n -> p (g n)"),
                )

        def values(j):
            p, wx, wc, wsc = state[j]
            if j % 2 == 0:
                y_bank = banks.tile([P, 2 * P], F32, name="y%d" % j, tag="b%d" % YB[j // 2], bufs=1)
                ybanks.append(y_bank)
            for g in range(2):
                cols = slice(g * P, (g + 1) * P)
                nc.tensor.matmul_mx(
                    out=ybanks[j // 2][:, j % 2 * P : (j % 2 + 1) * P],
                    lhsT=vc[:, cols].bitcast(FP8X4),
                    lhsT_scale=vsc[:, cols],
                    rhs=wc[:, cols].bitcast(FP8X4),
                    rhs_scale=wsc[:, cols],
                    start=(g == 0),
                    stop=(g == 1),
                )

        def normaliser(h):
            js = slice(2 * h, 2 * h + 2)
            nc.vector.reciprocal(rl[:, js], total[:, js])
            b = banks.tile([P, 256], F32, name="rlb%d" % h, tag="b%d" % RB[h], bufs=1)
            for i in range(2):
                c = 2 * h + i
                nc.tensor.transpose(b[:, i * P : (i + 1) * P], rl[:, c : c + 1].to_broadcast([P, P]), ident[:])
            nc.scalar.copy(rl_sb[:, h * 256 : (h + 1) * 256], b[:])

        def scatter(h):
            cols = slice(h * 256, (h + 1) * 256)
            nc.scalar.copy(y_sb[:, cols], ybanks[h][:])
            nc.vector.tensor_tensor(
                window[:].indirect(qlist[:, h * 16 : (h + 1) * 16]), y_sb[:, cols], rl_sb[:, cols], MULT
            )

        vb = keep.tile([P, T], BF16, name="vb")
        vg = keep.tile([P, N, 2], BF16, name="vg")
        vx = keep.tile([P, 2, DV, 4], BF16, name="vx", align_bytes=64)
        vc = keep.tile([P, 2 * DV], U32, name="vc", align_bytes=64)
        vsc = keep.tile([P, 2 * DV], U8, name="vsc", align_bytes=64)

        def load_values():
            for i in range(2):
                cols = slice(i * H, (i + 1) * H)
                nc.scalar.activation(vb[:, cols], vraw[:, cols], COPY)

        def gather_values():
            for g in range(2):
                nc.scalar.activation(
                    vg[:, g * 512 : (g + 1) * 512, 0], vb[:].indirect(slots[:, g * 32 : (g + 1) * 32]), COPY
                )
            b = banks.tile([P, 2, 4, DV], BF16, name="vt", tag="b%d" % VB, bufs=1)
            for g in range(2):
                for t in range(4):
                    nc.tensor.transpose(b[:, g, t, :], vg[:, g * 512 + t : (g + 1) * 512 : 4, 0], ident_bf16[:])
            nc.scalar.copy(vx[:], b[:].rearrange("p g t e -> p g e t"))

        scores(0)
        scores(1)
        load_values()
        scores_by_slot((2, 3,))
        scale_rows(0)
        stabiliser(0)
        weights(0)
        scale_rows(1)
        stabiliser(1)
        weights(1)
        gather_values()
        scale_rows(2)
        stabiliser(2)
        weights(2)
        scale_rows(3)
        stabiliser(3)
        weights(3)
        turn_and_scale(0)
        quantise_weights(0)
        nc.vector.quantize_mx(out=vc[:].bitcast(FP8X4), scales=vsc[:], in_=vx[:].rearrange("p g e t -> p (g e t)"))
        values(0)
        turn_and_scale(1)
        quantise_weights(1)
        values(1)
        turn_and_scale(2)
        quantise_weights(2)
        values(2)
        normaliser(0)
        turn_and_scale(3)
        normaliser(1)
        scatter(0)
        quantise_weights(3)
        values(3)
        scatter(1)
        nc.sync.dma_start(out, window[:])
